import numpy as np, ml_dtypes
CORES = [36,164,52,180,100,228,116,244]
N = 8
BF = ml_dtypes.bfloat16
A, W, HM, RO, MU = 1024, 2048, 2, 3, 4
n = A // 4
def view(j, c):
    return np.where(c < 0, W, (((c * (MU * j + 5)) >> 5) + 37 * j) & (W - 1))
def worth(tab, j, b):
    x = tab[:, view(j[None, :], b)]
    return np.add.reduce(np.maximum.accumulate(x[:, ::-1], axis=1)[:, ::-1], axis=0)
def pack(x, b, p):
    return {"sight": x.reshape(N, 128, W).astype(np.float32).astype(BF), "bun": np.ascontiguousarray(b.reshape(N, 128, A)).astype(np.int32), "pots": p.astype(np.int32)}
def looks(rng):
    return (rng.integers(0, 256, (N, 8, 16, W)) * rng.integers(1, 9, (N, 8, 1, W))) >> 3
def some(rng, goods, shares):
    return np.where(rng.random((N, 8, 16, A)) < rng.choice(np.array(shares), (N, 8, 1, A)), goods, -1)
def setup_inputs(rng):
    b = some(rng, rng.integers(0, 4096, (N, 8, 16, A)), [0.05, 0.2, 0.4, 0.7, 1.0])
    p = np.where(rng.random((N, 8, n)) < 0.85, rng.integers(0, 4096, (N, 8, n)), -1)
    return pack(looks(rng), b, p)
def setup_inputs_spread(rng):
    x = np.floor(np.exp2(8 * rng.random((N, 8, 1, W)) * rng.random((N, 8, 16, W)) ** 0.5)).astype(np.int64) - 1
    x = np.where(rng.random((N, 8, 16, W)) < 0.02, 255, np.clip(x, 0, 255))
    e = rng.choice(np.array([0.5, 1.0, 3.0, 6.0]), (N, 8, 1, A))
    b = some(rng, np.minimum((4096 * rng.random((N, 8, 16, A)) ** e).astype(np.int64), 4095), [0.05, 0.15, 0.5, 0.95])
    p = np.minimum((4096 * rng.random((N, 8, n)) ** rng.choice(np.array([0.3, 1.0, 4.0]), (N, 8, 1))).astype(np.int64), 4095)
    return pack(x, b, np.where(rng.random((N, 8, n)) < 0.9, p, -1))
def setup_inputs_ends(rng):
    see = view(np.arange(A), np.int64(4095))
    x = 255 * (rng.random((N, 8, 16, W)) < rng.choice(np.array([0.05, 0.3, 0.6, 0.95]), (N, 8, 1, W))).astype(np.int64)
    x[:, :, 0, see[0::4]] = 255
    far = np.array([0, A - 67, A - 66, A - 65, A - 4, A - 3, A - 2, A - 1]); x[..., see[far]] = 255
    b = some(rng, np.int64(4095), [0.0, 0.1, 0.5, 1.0])
    own = (rng.random((N, 8, 1, A)) < 0.33) & (np.arange(A) % 4 != 0)
    b = np.where(own, rng.integers(0, 4096, (N, 8, 16, A)), b)
    b[:, :, 3, 0::4] = 4095; b[..., 0] = 4095; b[..., A - 67:A - 64] = -1; b[..., A - 4] = -1
    end = np.where(rng.random((N, 8, 1, 3)) < 0.5, 4095, -1); end[N - 1, 7] = np.array([-1, 4095, -1]); end[0, 7] = np.array([-1, -1, 4095]); end[1, 7] = np.array([4095, -1, -1])
    b[..., A - 3:] = end
    p = np.where(rng.random((N, 8, n)) < 0.7, np.where(rng.random((N, 8, n)) < 0.6, 4095, -1), rng.integers(0, 4096, (N, 8, n)))
    p[..., 0] = 4095; p[..., n - 1] = 4095
    return pack(x, b, p)
def setup_inputs_corners(rng):
    x = looks(rng); b = rng.integers(0, 4096, (N, 8, 16, A)); p = rng.integers(0, 4096, (N, 8, n)); d = np.arange(16)[:, None]
    for r in range(N):
        mode = rng.permutation(8)
        for g in range(8):
            m = int(mode[g])
            if m == 0: b[r, g] = -1
            if m == 2: b[r, g, :15] = -1
            if m == 3: b[r, g, 1:] = -1
            if m == 4:
                c = int(b[r, g, 0, 0]); b[r, g] = np.where(rng.random((16, A)) < rng.random((1, A)), c, -1); p[r, g] = c
            if m == 5: b[r, g] = np.where(rng.random((1, A)) < 0.5, b[r, g], -1)
            if m == 6:
                k = rng.choice(np.array([0, 1, 15, 16]), (1, A)); low = rng.random((1, A)) < 0.5
                b[r, g] = np.where(np.where(low, d < k, d >= 16 - k), b[r, g], -1); p[r, g] = -1
            if m == 7: x[r, g] = 0
    return pack(x, b, p)
def calls(rng):
    return np.argsort(rng.random((N, 3, n)), axis=-1) + n * rng.integers(0, W // n, (N, 3, n))
def setup_inputs_ties(rng):
    base = rng.choice(np.array([0, 1, 127, 254]), (N, 8, 1, 1)); base[0, 0] = 0; base[0, 7] = 254; base[N - 1, 7] = 254
    x = base + (rng.random((N, 8, 16, W)) < 0.125)
    few = rng.integers(0, 4096, 32); few[0] = 0; few[1] = 4095
    b = some(rng, few[rng.integers(0, 32, (N, 8, 16, A))], [0.0, 0.1, 0.3, 0.6])
    p = np.where(rng.random((N, 8, n)) < 0.9, few[rng.integers(0, 32, (N, 8, n))], -1)
    full = rng.integers(0, 4096, (N, 16, A)); b3 = np.where(rng.random((N, 1, A)) < 0.5, full, -1)
    b3[:, :, 0::4] = full[:, :, 0::4]
    b3[:, 0:3, 0::4] = calls(rng)
    x[:, 3] = 100; b[:, 3] = b3
    for m in range(3):
        bm = rng.integers(0, 4096, (N, 16, A)); bm[:, 0:3, 0::4] = calls(rng); bm[:, :, m + 1::4] = -1
        x[:, 4 + m] = 100; b[:, 4 + m] = bm
    return pack(x, b, p)
def check_inputs(d):
    bad = []
    for k, lo, hi in (("sight", 0, 255), ("bun", -1, 4095), ("pots", -1, 4095)):
        v = np.asarray(d[k]).astype(np.float64)
        if not np.all((v >= lo) & (v <= hi) & (v == np.floor(v))): bad.append("range of " + k)
    return bad
def reference(sight, bun, pots):
    tab = np.zeros((N, 8, 16, W + 1), np.int32); tab[..., :W] = sight.astype(np.float32).reshape(N, 8, 16, W).astype(np.int32)
    bn = bun.astype(np.int64).reshape(N, 8, 16, A); p = pots.astype(np.int64); val = np.zeros((N, 8, A), np.int64)
    for r in range(N):
        for g in range(8): val[r, g] = worth(tab[r, g], np.arange(A), bn[r, g])[0]
    place = np.arange(16)[:, None]
    for t in range(RO):
        u = 4 * np.arange(n) + (t & 3); nbn = bn.copy(); nval = val.copy(); npots = np.zeros((N, 8, n), np.int64)
        for r in range(N):
            for g in range(8):
                old = bn[r, g][:, u]; s = old.copy(); s[15] = p[r, g]
                best = np.zeros(n, np.int64); who = np.full(n, -1); riv = []
                for m in range(3):
                    q = r if m < HM else (r + 1 + (t + m - HM) % (N - 1)) % N
                    j = 4 * ((old[m] + val[r, g, u] + 13 * t) & (n - 1)) + ((t + 1 + m) & 3)
                    first = np.zeros(n, bool); first[np.unique(j, return_index=True)[1]] = True
                    sv = worth(tab[q, g], j, s)
                    e = np.where(first, np.add.reduce((sv > val[q, g, j]).astype(np.int64), axis=0), 0)
                    who = np.where(e > best, m, who); best = np.maximum(best, e); riv.append((q, j, sv))
                new = s.copy()
                for m in range(3):
                    q, j, sv = riv[m]; c = np.flatnonzero(who == m); jc = j[c]
                    nbn[q, g][:, jc] = np.where(place >= best[c] - 1, s[:, c], -1); nval[q, g, jc] = sv[best[c] - 1, c]
                    new[:, c] = bn[q, g][:, jc]
                nbn[r, g][:, u] = new; nval[r, g, u] = worth(tab[r, g], u, new)[0]
                npots[(r + 1) % N, g] = np.where(best >= 2, s[np.maximum(best - 2, 0), np.arange(n)], old[15])
        bn, val, p = nbn, nval, npots
    return {"yb": bn.reshape(N, 128, A).astype(np.float32), "yv": val.astype(np.float32), "yp": p.astype(np.float32)}

from concourse.mybir import AluOpType as O, ActivationFunctionType as F

RO = 3
f32, b16, i32, u16 = "float32", "bfloat16", "int32", "uint16"
SCRATCH = {}


def _b(name, cols, dtype, where="sbuf"):
    SCRATCH[name] = (where, [128, cols], dtype)


for _k in range(8):
    _b("P%d" % _k, 512, f32, "psum")
for _n, _c, _d in [
    ("bunI", 1024, i32), ("potI", 256, i32), ("TB", 2064, b16), ("JC", 1024, f32), ("R01", 2048, b16),
    ("ip", 128, i32), ("ic", 128, i32), ("id0", 128, i32), ("q1", 128, i32), ("q2", 128, i32), ("q3", 128, i32),
    ("BM", 128, b16), ("BMq", 128, b16), ("BM8", 128, b16), ("DW", 128, b16), ("WX", 2048, b16), ("ONE", 256, b16),
    ("cr", 512, b16), ("zr", 128, b16), ("r15", 128, b16), ("thb", 256, b16), ("THR", 256, f32),
    ("SEL0", 128, f32), ("SEL1", 128, f32), ("SEL2", 128, f32), ("R15", 128, f32), ("NSH", 128, b16), ("BID", 128, b16),
    ("k1", 128, b16), ("k2", 128, b16), ("rmask", 8, f32), ("wk", 16, i32), ("I1", 16, f32), ("I16", 16, f32), ("I8", 16, f32),
    ("L0", 256, f32), ("V0L", 256, f32), ("BW", 12 * 256, f32), ("VW", 12 * 256, f32),
    ("UB1", 512, f32), ("VB1", 512, f32), ("UB2", 256, f32), ("VB2", 256, f32),
    ("P0in", 256, f32), ("Bz", 256, f32), ("DI", 256, i32), ("DIo", 256, i32), ("HB", 768, b16), ("Lf", 48, f32),
    ("LV", 32, u16), ("p01", 32, f32), ("EB", 6528, b16), ("D8", 512, b16), ("D01", 512, b16),
    ("VJ0", 256, f32), ("VJ1", 256, f32), ("VJ2", 256, f32), ("SMb", 8192, b16), ("SM2", 4096, b16), ("SMo", 4096, b16),
    ("CM0", 512, b16), ("CM1", 256, b16), ("CMB", 256, b16), ("E02", 32, f32),
    ("dec", 512, f32), ("IDX", 32, u16), ("Ys", 256, f32), ("SMg", 256, b16), ("VN", 256, f32), ("SMg2", 256, b16), ("VN2", 256, f32),
    ("X2i", 32, u16), ("OFFO", 256, u16), ("OFFI", 1024, u16), ("OUT", 1024, f32), ("OUTV", 1024, f32), ("PO", 256, f32),
]:
    _b(_n, _c, _d)
_b("GR", 4 * 4096, b16)
for _k in range(4):
    _b("h1_%d" % _k, 256, i32)
for _k in range(3):
    _b("h2_%d" % _k, 256, i32)
for _k in range(2):
    _b("OFF%d" % _k, 256, u16)
for _k in range(RO):
    _b("OS%d" % _k, 272, u16)
    _b("OL%d" % _k, 272, u16)
    _b("CS%d" % _k, 256, f32)
    _b("KS%d" % _k, 256, b16)
    _b("KL%d" % _k, 256, b16)
    _b("XS%d" % _k, 288, f32)
    _b("XL%d" % _k, 288, f32)
    _b("PS%d" % _k, 256, f32)
    _b("PL%d" % _k, 256, f32)
SEMAPHORES = ["v", "s", "t", "gp", "ls"] + ["d%d" % k for k in range(10)] + ["%s%d" % (n, k) for n in ("ro", "rc", "rk", "rx", "rp") for k in range(RO)]
CP = {"cy": 1.0e-3, "pe": 0.75e-3, "gat": 1.5, "sca": 3.5, "rem": 3.2, "lat": 0.15}
BOOST = {'g0': 16.1, 'rk': 6.3, 'rp': 4.0, 'dd1': -2.3, 'ol0': 12.0, 'ol1': 19.3, 'io': 11.4, 'rx': 19.1, 'g2': 18.4, 'j11': 2.3, 'vj2': 13.6, 'rc': -7.1, 'cs': 7.4, 'ro': 6.3, 'dec0': 0.4, 'dd2': -1.0, 'const': -6.2, 'c0': 2.7, 'look0': 6.8, 'sc1': 9.8, 'j2': -1.1, 'dec1': -0.3, 'out': 1.6, 'init': 1.3, 'vj1': 4.3, 'look1': 0.6, 'own': 0.6, 'j10': 2.0, 'hc': -2.2}
_order = {}


def needs(ops):
    n = len(ops)
    dep = [set() for _ in range(n)]
    hist = {}
    for i, o in enumerate(ops):
        if o["after"] is not None:
            dep[i].add(o["after"])
        for lst, w in ((o["ins"], False), (o["outs"], True)):
            for x in lst:
                nm, lo, hi = x[1], x[2], x[3]
                if nm is None:
                    continue
                ps = SCRATCH[nm][0] == "psum" if nm in SCRATCH else False
                for (l, h, w2, k) in hist.get(nm, ()):
                    if k != i and ((w or w2) and l < hi and h > lo or ps and ops[k]["q"] != o["q"]):
                        dep[i].add(k)
        for lst, w in ((o["ins"], False), (o["outs"], True)):
            for x in lst:
                nm, lo, hi = x[1], x[2], x[3]
                if nm is None:
                    continue
                if w:
                    hist[nm] = [r for r in hist.get(nm, []) if not (r[0] >= lo and r[1] <= hi)]
                hist.setdefault(nm, []).append((lo, hi, w, i))
    return dep


def arrange(ops, dep):
    n = len(ops)
    suc = [[] for _ in range(n)]
    for i in range(n):
        for k in dep[i]:
            suc[k].append(i)
    pr = [0.0] * n
    for i in range(n - 1, -1, -1):
        pr[i] = ops[i]["cost"] + ops[i]["lat"] + max([pr[k] for k in suc[i]] + [0.0]) + BOOST.get(ops[i]["tag"], 0.0)
    left = [len(d) for d in dep]
    rdy = [0.0] * n
    free = {}
    pool = {}
    for i in range(n):
        if not left[i]:
            pool.setdefault(ops[i]["q"], []).append(i)
    order = []
    while len(order) < n:
        best = None
        for q, c in pool.items():
            if not c:
                continue
            f = free.get(q, 0.0)
            t = max(f, min(rdy[i] for i in c))
            if best is None or t < best[0]:
                k = max((i for i in c if rdy[i] <= t + 1e-9), key=lambda i: pr[i])
                best = (t, q, k)
        t, q, i = best
        pool[q].remove(i)
        order.append(i)
        end = t + ops[i]["cost"]
        free[q] = end if q != "R" else 0.0
        for k in suc[i]:
            rdy[k] = max(rdy[k], end + ops[i]["lat"])
            left[k] -= 1
            if not left[k]:
                pool.setdefault(ops[k]["q"], []).append(k)
    return order


def rank_program(g, core, T, topo):
    rank = T.rank_of(core)
    if rank is None:
        return
    N = len(T.cores)
    eng = {"V": g.vector, "S": g.scalar, "T": g.tensor, "Y": g.sync, "G": g}
    own = {"V": "v", "S": "s", "T": "t", "G": "gp"}
    cnt = {"v": 0, "s": 0, "t": 0, "gp": 0, "ls": 0}
    know = {q: {} for q in eng}
    recs = {}
    nd = [0]
    tag = [""]
    ops = []
    sent = {}

    def A(n, lo=0, hi=None, st=1, ps=slice(None)):
        if hi is None:
            hi = T[n].shape[1]
        return (T[n][ps, lo:hi:st], n, lo, hi)

    def cols(x):
        return x[0].shape[1]

    def IND(w, o):
        return (w[0].indirect(o[0]), [w, o])

    def flat(lst):
        out = []
        for o in lst:
            if isinstance(o[1], list):
                out += o[1]
            else:
                out.append(o)
        return out

    def add(q, fns, outs, ins, cost, lat=None, after=None, kind="c"):
        ops.append({"q": q, "fns": fns, "outs": flat(outs), "ins": flat(ins), "cost": cost, "lat": CP["lat"] if lat is None else lat,
                    "after": after, "kind": kind, "tag": tag[0]})

    def two(x):
        return SCRATCH[x[1]][2] in (b16, u16)

    def psum(x):
        return SCRATCH[x[1]][0] == "psum"

    def tt(o, a, b, op):
        if isinstance(a[1], list):
            c = 0.06 + 16 * cols(a[1][1]) * CP["gat"] * CP["cy"]
        else:
            c = max(64, cols(a) * (1 if psum(a) or psum(b) else 2)) * CP["cy"]
        add("V", [lambda: g.vector.tensor_tensor(o[0], a[0], b[0], op)], [o], [a, b], c)

    def ts(o, a, s1, op0, s2=None, op1=None):
        x = [a] + [s for s in (s1,) if isinstance(s, tuple)]
        v1 = s1[0] if isinstance(s1, tuple) else s1
        c = max(64, cols(a) * (0.5 if two(o) and two(a) else 1)) * CP["cy"]
        if op1 is None:
            add("V", [lambda: g.vector.tensor_scalar(o[0], a[0], v1, None, op0)], [o], x, c)
        else:
            add("V", [lambda: g.vector.tensor_scalar(o[0], a[0], v1, s2, op0, op1)], [o], x, c)

    def cp(o, a):
        if isinstance(o[1], list):
            c = 0.06 + 16 * cols(o[1][1]) * CP["sca"] * CP["cy"]
        elif isinstance(a[1], list):
            c = 0.06 + 16 * cols(a[1][1]) * CP["gat"] * CP["cy"]
        else:
            c = max(64, cols(a) * (0.5 if two(o) and two(a) else 1)) * CP["cy"]
        add("V", [lambda: g.vector.tensor_copy(o[0], a[0])], [o], [a], c)

    def fill(o, c):
        add("V", [lambda: g.vector.memset(o[0], c)], [o], [], max(64, cols(o) * (0.5 if two(o) else 1)) * CP["cy"])

    def act(o, a, scale=1.0):
        c = 0.07 + 16 * cols(a[1][1]) * CP["gat"] * CP["cy"] if isinstance(a[1], list) else 0.1 + cols(a) * CP["cy"]
        if isinstance(scale, tuple):
            add("S", [lambda: g.scalar.activation(o[0], a[0], F.Copy, 0.0, scale[0])], [o], [a, scale], c)
        else:
            add("S", [lambda: g.scalar.activation(o[0], a[0], F.Copy)], [o], [a], c)

    def mms(lst):
        def one(x):
            return lambda: g.tensor.matmul(x[0][0], x[1][0], x[2][0], x[3], x[4])
        c = sum(max(64, cols(x[2])) * (1 if two(x[1]) else 4) for x in lst) * CP["pe"]
        add("T", [one(x) for x in lst], [x[0] for x in lst], [y for x in lst for y in x[1:3]], c)

    def mm(o, l, r, s, e):
        mms([(o, l, r, s, e)])

    def iota(o, pat, base, cm):
        c = 0.15 + 2 * cols(o) * CP["cy"]
        if SCRATCH[o[1]][2] != i32:
            add("G", [lambda: g.iota(o[0], pat, base, cm, allow_small_or_imprecise_dtypes=True)], [o], [], c)
        else:
            add("G", [lambda: g.iota(o[0], pat, base, cm)], [o], [], c)

    def dma(q, out, in_):
        tag[0] = "io"
        add(q, [lambda: eng[q].dma_start(out[0], in_[0])], [out] if out[1] else [], [in_] if in_[1] else [], 0.1, 3.0, None, "d")

    def send(dst, out, in_, sem):
        m = topo.mask(core, dst)
        rid, pid = topo.addr(dst, core)
        cnt["ls"] += len(topo.engines(core, dst))
        sent[sem] = len(ops)
        add("G", [lambda: g.remote_dma(out[0], in_[0], T.sem[sem], T.sem.ls, pid, rid, m)], [], [in_], 0.4, 0.0, None, "r")
        ops[-1]["tag"] = sem[:2]

    def recv(out, sem, src):
        ne = len(topo.engines(src, core))
        add("R", [(sem, ne)], [out], [], 0.0, CP["rem"], sent[sem], "v")

    def wait_for(q, outs, ins):
        need = []
        for lst, w in ((ins, False), (outs, True)):
            for o in lst:
                n, lo, hi = o[1], o[2], o[3]
                if n is None:
                    continue
                ps = SCRATCH[n][0] == "psum" if n in SCRATCH else False
                for r in recs.get(n, ()):
                    if r[3] == q:
                        if q == "T" and ps:
                            continue
                        if (w or r[2]) and r[0] < hi and r[1] > lo:
                            need.append(r)
                    elif ps:
                        need.append(r)
                    elif r[0] < hi and r[1] > lo and (w or r[2]):
                        need.append(r)
        kn = know[q]
        need = [r for r in need if kn.get(r[4], 0) < r[5]]
        need.sort(key=lambda r: -sum(r[6].values()))
        for r in need:
            if kn.get(r[4], 0) < r[5]:
                eng[q].wait_ge(T.sem[r[4]], r[5])
                for s, v in r[6].items():
                    if kn.get(s, 0) < v:
                        kn[s] = v

    def note(n, lo, hi, w, q, sem, val, clk):
        if n is None:
            return
        if w:
            recs[n] = [r for r in recs.get(n, []) if not (r[0] >= lo and r[1] <= hi)]
        recs.setdefault(n, []).append((lo, hi, w, q, sem, val, clk))

    def issue(o):
        q = o["q"]
        if o["kind"] == "v":
            sem, ne = o["fns"][0]
            cnt[sem] = ne
            x = o["outs"][0]
            note(x[1], x[2], x[3], True, "R", sem, ne, {sem: ne})
            return
        wait_for(q, o["outs"], o["ins"])
        if o["kind"] == "r":
            o["fns"][0]()
            return
        if o["kind"] == "d":
            s, by = "d%d" % nd[0], "D"
            nd[0] += 1
            cnt[s] = 16
            o["fns"][0]().then_inc(T.sem[s], 16)
        else:
            s, by = own[q], q
            for f in o["fns"]:
                cnt[s] += 1
                f().then_inc(T.sem[s], 1)
        clk = dict(know[q])
        clk[s] = cnt[s]
        for x in o["ins"]:
            note(x[1], x[2], x[3], False, by, s, cnt[s], clk)
        for x in o["outs"]:
            note(x[1], x[2], x[3], True, by, s, cnt[s], clk)

    def pull(off, lo, n, q="S", kind=0, at=None):
        k = 4096 * kind + 16 * (lo if at is None else at)
        o, w = A("GR", k, k + 16 * n), IND(A("TB"), A(off, lo, lo + n))
        if q == "S":
            act(o, w)
        else:
            cp(o, w)
        return k

    def scan(n, lo, k, m):
        e = lo + 16 * m
        o = (T[n][:, e - 1:(lo - 1 if lo else None):-1], n, lo, e)
        d = (T.GR[:, k + 16 * m - 1:(k - 1 if k else None):-1], "GR", k, k + 16 * m)
        z = (T.R01[:, 16 * m - 1::-1], "R01", 0, 16 * m)
        add("V", [lambda: g.vector.tensor_tensor_scan(o[0], z[0], d[0], 0.0, O.mult, O.max)], [o], [z, d], 8 * m * CP["cy"])

    dma("Y", A("bunI"), (T.bun[:], None, 0, 0))
    dma("S", A("TB", 37, 2048), (T.sight[:, 0:2011], None, 0, 0))
    dma("S", A("TB", 0, 37), (T.sight[:, 2011:2048], None, 0, 0))
    fill(A("potI"), -1)
    dma("Y", (T.potI[15::16, :], "potI", 0, 256), (T.pots[:], None, 0, 0))
    iota(A("JC"), [[1, 4], [4, 256]], 1, 0)
    iota(A("ip"), [[0, 128]], 0, 1)
    iota(A("ic"), [[1, 128]], 0, 0)
    iota(A("id0"), [[-1, 128]], 0, 1)
    iota(A("wk"), [[16, 16]], 0, 0)
    tag[0] = "const"
    fill(A("TB", 2048, 2064), 0.0)
    fill(A("R01"), 1.0)
    fill(A("R01", 15, 2048, 16), 0.0)
    fill(A("ONE"), 1.0)
    fill(A("WX"), 0.0)
    for y in range(16):
        fill(A("thb", y, 256, 16), 2.0 ** -y)
    for s in range(4):
        fill(A("cr", 128 * s, 128 * s + 128), float(s + 1))
    fill(A("zr"), 0.0)
    fill(A("r15"), 0.0)
    fill(A("r15", 15, 128, 16), 1.0)
    ts(A("q1"), A("ip"), 4, O.arith_shift_right)
    ts(A("q2"), A("ic"), 4, O.arith_shift_right)
    tt(A("BM"), A("q1"), A("q2"), O.is_equal)
    ts(A("q3"), A("ip"), 15, O.bitwise_and)
    for gg in range(8):
        ts(A("WX", 16 * gg, 16 * gg + 15 * 129 + 1, 129), A("ONE", 0, 16), A("BM", 16 * gg, 16 * gg + 1), O.mult)

    def W(y):
        return A("WX", 128 * y, 128 * y + 128)

    ts(A("BMq"), A("BM"), 0.25, O.mult)
    ts(A("BM8"), A("BM"), 8.0, O.mult)
    for m in range(3):
        ts(A("k1"), A("q3"), m, O.is_equal)
        tt(A("SEL%d" % m), A("k1"), A("BM"), O.mult)
    ts(A("rmask", 0, 1), A("q3", 0, 1), 15, O.not_equal)
    cp(A("R15"), W(15))
    ts(A("k1"), A("id0"), 1, O.is_equal)
    tt(A("k1"), A("k1"), A("BM"), O.mult)
    ts(A("NSH"), A("k1"), -1.0, O.mult)
    ts(A("k2"), A("id0"), 2, O.is_equal)
    tt(A("k2"), A("k2"), A("BM"), O.mult)
    tt(A("k1"), A("k1"), A("k2"), O.subtract)
    ts(A("k2"), A("q3"), 1, O.is_equal)
    tt(A("k2"), A("k2"), W(15), O.mult)
    tt(A("BID"), A("k1"), A("k2"), O.subtract)
    tt(A("I1"), A("q3", 0, 16), A("wk"), O.add)
    ts(A("I16"), A("I1"), 16.0, O.mult)
    for h in range(2):
        cp(A("I8", 8 * h, 8 * h + 8), A("I16", 0, 8))
    ts(A("THR"), A("thb"), 2.0, O.mult)
    mm(A("P4", 0, 128), A("thb", 0, 128, 1, slice(0, 1)), A("ONE", 0, 128, 1, slice(0, 1)), True, True)
    tt(A("DW"), A("P4", 0, 128), A("BM"), O.mult)
    ONE1 = A("ONE", 0, 256, 1, slice(0, 1))
    ONEh = A("ONE", 0, 128, 1, slice(0, 1))
    iota(A("BW", 1536, 1792), [[0, 256]], 0, 0)
    iota(A("BW", 2304, 2560), [[0, 256]], 0, 0)

    def goods(o, src, pt):
        ts(pt, src, 0, O.is_ge, 296.0, O.mult)
        tt(o, pt, src, O.add)

    def look(o, D, c, J, k):
        h1 = A("h1_%d" % k, 0, cols(c))
        tt(h1, c, J, O.mult)
        tt(h1, h1, D, O.add)
        ts(h1, h1, 3, O.arith_shift_right, 2047 | (1 << 20), O.bitwise_and)
        ts(o, h1, 2048, O.min)

    def quarter(o, c):
        ts(o, c, 0.25, O.mult, -74.375, O.add)

    def worth(off, lo, dst, at, n, q="S"):
        tag[0] = "own"
        k = pull(off, lo, n, q, 3, at)
        scan("SMo", 16 * at, k, n)
        mm(A("P7", at, at + n), A("BM"), A("SMo", 16 * at, 16 * at + 16 * n, 16), True, True)
        act(dst, A("P7", at, at + n))

    BWc = {1: ("BW", 512), 2: ("BW", 768), 3: ("BW", 1792), 0: ("L0", 0)}
    VWc = {1: ("VW", 512), 2: ("VW", 768), 3: ("VW", 1792), 0: ("V0L", 0)}

    def sub(x, lo, hi):
        return A(x[0], x[1] + lo, x[1] + hi)
    act(A("P5"), A("JC", 0, 512))
    act(A("P6"), A("JC", 512, 1024))
    tag[0] = "init"
    for s in range(4):
        goods(sub(BWc[s], 0, 256), A("bunI", s, 1024, 4), A("P%d" % s, 0, 256))
        quarter(A("DIo"), sub(BWc[s], 0, 256))
        look(A("OFFI", 256 * s, 256 * s + 256), A("DIo"), sub(BWc[s], 0, 256), A("P%d" % (5 + s // 2), 256 * (s % 2), 256 * (s % 2) + 256), s)
    goods(A("P0in"), A("potI"), A("P4", 0, 256))

    def first_worth(s):
        for h in range(2):
            worth("OFFI", 256 * s + 128 * h, sub(VWc[s], 128 * h, 128 * h + 128), 128 * h, 128)
    first_worth(0)
    first_worth(1)

    wins = [(0, 1024, 0, 512, 768), (768, 2048, 256, 0, 1024), (1792, 3072, 768, 0, 256)]
    Sblk = [0, 1024, 2560]
    hostw = [("BW", "VW", 1536, 2048, 256, 0), ("BW", "VW", 2048, 2560, 0, 256), ("UB1", "VB1", 0, 512, 0, 256)]
    lead = [(("L0", 0), ("V0L", 0)), (("BW", 512), ("VW", 512)), (("BW", 768), ("VW", 768))]
    newl = [(("BW", 2048), ("VW", 2048)), (("UB1", 0), ("VB1", 0)), (("UB2", 0), ("VB2", 0))]
    nxt, prv = T.cores[(rank + 1) % N], T.cores[(rank - 1) % N]

    def DC(k, w=16):
        return A("dec", 16 * k, 16 * k + w)

    def wrap(at, src, lo, k0=0, k1=16):
        mms([(A("P6", at + k0, at + k1), W(y), A(src, lo + 16 * k0 + y, lo + 16 * k1, 16), y == 0, y == 15) for y in range(16)])

    def judge(bank, at, smn, lo, n, k):
        scan(smn, lo, k, n)
        mms([(A(bank, at, at + n), W(d), A(smn, lo + d, lo + 16 * n, 16), d == 0, d == 15) for d in range(16)])

    def dedup(m):
        base = 2176 * m
        o = [base + sum(256 - 16 * j for j in range(k)) for k in range(17)]
        for k in range(16):
            ts(A("EB", o[k], o[k + 1]), A("HB", 256 * m + 16 * k, 256 * m + 256), A("Lf", 16 * m + k, 16 * m + k + 1), O.is_equal)
        P = "P%d" % m
        l = [(A(P, 0, 256), A("zr", 0, 128, 1, slice(0, 1)), ONE1, True, False)]
        for k in range(16):
            if k < 15:
                l.append((A(P, 16 * k + 16, 256), A("BM8"), A("EB", o[k] + 16, o[k + 1]), False, False))
            l.append((A(P, 16 * k, 16 * k + 16), A("DW"), A("EB", o[k], o[k] + 16), False, k == 15))
        for a in range(0, len(l), 4):
            mms(l[a:a + 4])

    def host_change(t):
        bw, vw, a, e, cb, db = hostw[t]
        recv(A("XL%d" % t), "rx%d" % t, T.cores[(rank - 1 - t) % N])
        tag[0] = "hc"
        cp(A("X2i"), A("XL%d" % t, 256, 288))
        act(A("SMg2"), IND(A("SM2"), A("X2i", 16, 32)))
        mm(A("P7", 256, 512), A("BM"), A("SMg2"), True, True)
        act(A("VN2"), A("P7", 256, 512))
        cp(IND(A(bw, a, e), A("X2i", 0, 16)), A("XL%d" % t, 0, 256))
        cp(IND(A(vw, a, e), A("X2i", 0, 16)), A("VN2"))

    for t in range(RO):
        q, p = T.cores[(rank + 1 + t) % N], T.cores[(rank - 1 - t) % N]
        LB, LVv = sub(lead[t][0], 0, 256), sub(lead[t][1], 0, 256)
        wa, we, so, c0, c1 = wins[t]
        S = A("BW", Sblk[t], Sblk[t] + 256)
        if t == 0:
            pool = A("P0in")
        else:
            pool = A("PL%d" % (t - 1))
            recv(pool, "rp%d" % (t - 1), prv)
        tag[0] = "hash"
        ts(A("Bz"), LB, 39.0, O.max, 13.0 * t + 216.0, O.add)
        act(A("P5", 0, 256), LB, A("rmask", 0, 1))
        for m in (0, 2, 1):
            h1, h2, HBm = A("h1_%d" % m), A("h2_%d" % m), A("HB", 256 * m, 256 * m + 256)
            P = "P%d" % m
            mm(A(P, 0, 256), A("SEL%d" % m), A("Bz"), True, True)
            tt(h1, A(P, 0, 256), LVv, O.add)
            ts(h2, h1, 255, O.bitwise_and)
            cp(HBm, h2)
            s = (t + 1 + m) & 3
            mms([(A(P, 256, 512), A("cr", 128 * s, 128 * s + 128, 1, slice(0, 1)), ONE1, True, False),
                 (A(P, 256, 512), A("BMq"), HBm, False, True)])
        tt(S, A("P5", 0, 256), pool, O.max)
        quarter(A("DI"), S)
        PD = A("P5", 256, 512)
        mms([(A("P6", 0, 48), W(y), A("HB", y, 768, 16), y == 0, y == 15) for y in range(16)])
        ts(A("Lf"), A("P6", 0, 48), 0.0625, O.mult)
        cp(PD, A("DI"))
        OS, OL = "OS%d" % t, "OL%d" % t
        for m in (0, 2, 1):
            J = A("P%d" % m, 256, 512)
            tag[0] = "look%d" % m
            look(A(OS, 0, 256) if m == 2 else A("OFF%d" % m), PD, S, J, m)
            if m == 2:
                cp(A(OS, 256, 272), A("Lf", 32, 48))
                send(q, A(OL), A(OS), "ro%d" % t)
        tag[0] = "g0"
        k0 = [pull("OFF0", 128 * h, 128) for h in range(2)]
        ts(A("p01", 0, 16), A("Lf", 0, 16), float(c0), O.add)
        ts(A("p01", 16, 32), A("Lf", 16, 32), float(c1), O.add)
        cp(A("LV"), A("Lf", 0, 32))
        tag[0] = "dd0"
        dedup(0)
        tag[0] = "j0"
        for h in range(2):
            judge("P3", 128 * h, "SMb", 4096 * h, 128, k0[h])
        if t == 0:
            first_worth(3)
        bw, vw, ha, he, hcb, hdb = hostw[t]
        recv(A(OL), "ro%d" % t, p)
        tag[0] = "cs"
        clsB, clsV = A(bw, ha + hcb, ha + hcb + 256), A(vw, ha + hcb, ha + hcb + 256)
        act(A("CS%d" % t), IND(clsB, A(OL, 256, 272)))
        send(p, A("BW", Sblk[t] + 256, Sblk[t] + 512), A("CS%d" % t), "rc%d" % t)
        tag[0] = "g2"
        k2 = [pull(OL, 128 * h, 128, "S", 2) for h in range(2)]
        tag[0] = "vj2"
        act(A("VJ2"), IND(clsV, A(OL, 256, 272)))
        tag[0] = "c0"
        tt(A("D01", 0, 256), A("P0", 0, 256), A("THR"), O.is_ge)
        ts(A("D8", 0, 256), A("D01", 0, 256), 8192.0, O.mult)
        tt(A("VJ0"), IND(A("VW", wa + c0, wa + c0 + 256), A("LV", 0, 16)), A("D8", 0, 256), O.add)
        tt(A("CM0", 0, 256), A("P3", 0, 256), A("VJ0"), O.is_gt)
        act(A("P0", 0, 256), A("CM0", 0, 256))
        if t > 0:
            host_change(t - 1)
        tag[0] = "j2"
        for h in range(2):
            judge("P5", 128 * h, "SM2", 2048 * h, 128, k2[h])
        tt(A("KS%d" % t), A("P5", 0, 256), A("VJ2"), O.is_gt)
        send(p, A("KL%d" % t), A("KS%d" % t), "rk%d" % t)
        tag[0] = "dd1"
        dedup(1)
        tag[0] = "dd2"
        dedup(2)
        tt(A("D01", 256, 512), A("P1", 0, 256), A("THR"), O.is_ge)
        ts(A("D8", 256, 512), A("D01", 256, 512), 8192.0, O.mult)
        if t == 0:
            first_worth(2)
        tag[0] = "vj1"
        tt(A("VJ1"), IND(A("VW", wa + c1, wa + c1 + 256), A("LV", 16, 32)), A("D8", 256, 512), O.add)
        tt(A("P2", 256, 512), A("P2", 0, 256), A("THR"), O.is_lt)
        recv(A("KL%d" % t), "rk%d" % t, q)
        tag[0] = "pre"
        tt(A("CM0", 256, 512), A("KL%d" % t), A("P2", 256, 512), O.mult)
        mms([(A("P6", 64, 96), W(y), A("CM0", y, 512, 16), y == 0, y == 15) for y in range(16)])
        tt(A("P0", 0, 256), A("P0", 0, 256), A("CM0", 256, 512), O.max)
        act(A("E02"), A("P6", 64, 96))
        e0, e2 = A("E02", 0, 16), A("E02", 16, 32)
        ts(DC(0), e0, 1.0, O.add)
        tt(DC(0), DC(0), e2, O.max)
        ts(DC(2), e0, 0.0, O.is_gt)
        ts(DC(1), A("I1"), float(so), O.add)
        tt(DC(3), A("p01", 0, 16), DC(1), O.subtract)
        tt(DC(3), DC(3), DC(2), O.mult)
        tt(DC(3), DC(3), DC(1), O.add)
        tt(DC(4), e2, e0, O.is_gt)
        ts(DC(1), DC(1), 256.0, O.add)
        tt(DC(5), DC(1), DC(3), O.subtract)
        tt(DC(5), DC(5), DC(4), O.mult)
        tt(DC(5), DC(5), DC(3), O.add)
        tt(DC(6), A("p01", 16, 32), DC(5), O.subtract)
        ts(DC(7), e0, -1.0, O.add, 0.0, O.max)
        tt(DC(7), DC(7), A("I8"), O.add)
        tt(DC(8), A("I8"), DC(7), O.subtract)
        ts(DC(8), DC(8), 2047.0, O.add)
        ts(DC(9), A("I1"), float(hdb), O.add)
        tt(DC(10), A("Lf", 32, 48), DC(9), O.subtract)
        ts(DC(10), DC(10), float(hcb), O.add)
        tt(DC(10), DC(10), DC(4), O.mult)
        tt(DC(9), DC(9), DC(10), O.add)
        ts(DC(11), e2, -1.0, O.add, 0.0, O.max)
        XS = "XS%d" % t
        tt(A(XS, 272, 288), DC(11), A("I16"), O.add)
        win = A("BW", wa, we)
        recv(A("BW", Sblk[t] + 256, Sblk[t] + 512), "rc%d" % t, q)
        for h in range(2):
            lo, hi, bank, fb = 128 * h, 128 * h + 128, ("P4", "P5")[h], ("P3", "P4")[h]
            at = lo
            tag[0] = "j1%d" % h
            for n in ([128], [64, 64])[h]:
                judge(bank, at - lo, "SMb", 2048 + 2048 * h + 16 * at, n, pull("OFF1", at, n, "S", 1))
                at += n
            H = lambda k: A("dec", 16 * k + 8 * h, 16 * k + 8 * h + 8)
            tag[0] = "dec%d" % h
            tt(A("CM1", lo, hi), A(bank, 0, 128), A("VJ1", lo, hi), O.is_gt)
            wrap(96, "CM1", 0, 8 * h, 8 * h + 8)
            tt(A("CMB", lo, hi), A("P0", lo, hi), A("CM1", lo, hi), O.max)
            mms([(A(fb, 256, 384), A("r15", 0, 128, 1, slice(0, 1)), ONEh, True, False),
                 (A(fb, 256, 384), A("BID"), A("CMB", lo, hi), False, True),
                 (A(fb, 384, 512), A("ONE", 0, 128, 1, slice(0, 1)), ONEh, True, False),
                 (A(fb, 384, 512), A("NSH"), A("CMB", lo, hi), False, True)])
            E1 = A("P6", 96 + 8 * h, 104 + 8 * h)
            j = 16 * (13 + h)
            d13, d14 = A("dec", j, j + 8), A("dec", j + 8, j + 16)
            tt(H(12), E1, H(0), O.is_ge)
            tt(d14, E1, H(8), O.add)
            tt(d13, H(12), H(6), O.mult)
            tt(d14, d14, H(12), O.mult)
            tt(d13, d13, H(5), O.add)
            tt(d14, d14, H(7), O.add)
            cp(A("IDX", 16 * h, 16 * h + 16), A("dec", j, j + 16))
            iu, iv = A("IDX", 16 * h, 16 * h + 8), A("IDX", 16 * h + 8, 16 * h + 16)
            U = sub(newl[t][0], lo, hi)
            act(U, IND(win, iu))
            act(A("SMg", lo, hi), IND(A("SMb", 4096 * h, 4096 * h + 4096), iv))
            mm(A("P7", 256 + lo, 256 + hi), A("BM"), A("SMg", lo, hi), True, True)
            tt(A("Ys", lo, hi), A(fb, 256, 384), sub(lead[t][0], lo, hi), O.mult)
            mm(A("P6", 256 + lo, 256 + hi), A("R15"), A("Ys", lo, hi), True, True)
            act(A("PS%d" % t, lo, hi), A("P6", 256 + lo, 256 + hi))
            tt(A(XS, lo, hi), A(fb, 384, 512), A("BW", Sblk[t] + lo, Sblk[t] + hi), O.mult)
            act(A("VN", lo, hi), A("P7", 256 + lo, 256 + hi))
            tag[0] = "sc%d" % h
            cp(IND(win, iu), A(XS, lo, hi))
            cp(IND(A("VW", wa, we), iu), A("VN", lo, hi))
            if h == 1:
                send(nxt, A("PL%d" % t), A("PS%d" % t), "rp%d" % t)
                tt(DC(12), DC(12), DC(10), O.mult)
                tt(A(XS, 256, 272), DC(9), DC(12), O.subtract)
                send(q, A("XL%d" % t), A(XS), "rx%d" % t)
            tag[0] = "ol%d" % h
            quarter(A("DIo", lo, hi), U)
            look(A("OFFO", lo, hi), A("DIo", lo, hi), U, A("JC", 256 * t + lo, 256 * t + hi), 3)
            for a in (lo, lo + 64) if t + 1 == RO else (lo,):
                n = 64 if t + 1 == RO else 128
                worth("OFFO", a, sub(newl[t][1], a, a + n), a, n, "V" if t + 1 == RO and a % 128 else "S")

    recv(A("PL%d" % (RO - 1)), "rp%d" % (RO - 1), prv)
    host_change(RO - 1)
    fb = {0: newl[0][0], 1: newl[1][0], 2: newl[2][0], 3: ("BW", 1792)}
    fv = {0: newl[0][1], 1: newl[1][1], 2: newl[2][1], 3: ("VW", 1792)}
    tag[0] = "out"
    ts(A("PO"), A("PL%d" % (RO - 1)), -296.0, O.add, -1.0, O.max)
    dma("Y", (T.yp[:], None, 0, 0), (T.PO[15::16, :], "PO", 0, 256))
    for s in range(4):
        ts(A("OUT", s, 1021 + s, 4), sub(fb[s], 0, 256), -296.0, O.add, -1.0, O.max)
        act(A("OUTV", s, 1021 + s, 4), sub(fv[s], 0, 256))
    dma("Y", (T.yb[:], None, 0, 0), A("OUT"))
    dma("Y", (T.yv[:], None, 0, 0), (T.OUTV[0::16, :], "OUTV", 0, 1024))

    if not _order:
        _order["o"] = arrange(ops, needs(ops))
    for i in _order["o"]:
        issue(ops[i])
    for s in sorted(cnt):
        if cnt[s]:
            g.wait_ge(T.sem[s], cnt[s])
